import numpy as np, ml_dtypes
CORES = [21,85,149,213,277,341,405,469]
N = 8
T, CAP = 2048, 256
def entries(a): return a.T.reshape(-1)
def pack(v, P): return np.ascontiguousarray(np.asarray(v, np.int32).reshape(-1, P).T)
def lists(rng, how):
    n = rng.integers(0, CAP + 1, (N, 8))
    if how in ("comb", "full"): n[:] = CAP
    if how == "one": n[:] = 1
    if how == "none": n[int(rng.integers(N))] = 0; n[:, int(rng.integers(8))] = 0
    F = np.zeros((N, 8, T), np.int64)
    for r in range(N):
        for h in range(8):
            o = (rng.permutation(16)[:, None] + 16 * np.arange(T // 16)).reshape(-1) if how == "comb" else rng.permutation(T)
            F[r, h, o[:n[r, h]]] = 1
    if how == "run":
        p = rng.permutation(8); n[:, p[:2]] = CAP; n[:, p[2]] = CAP * rng.permutation(np.arange(N) % 2); n[:, p[3]] = 0
        s = rng.integers(0, T - n + 1); s[:, p[0]] = 0; s[:, p[1]] = T - CAP; s[:, p[2]] = 16 * rng.integers(0, max(1, (T - CAP) // 16), N) + 1
        F = ((np.arange(T) >= s[:, :, None]) & (np.arange(T) < (s + n)[:, :, None])).astype(np.int64)
    return {"keep": np.stack([np.concatenate([pack(F[r, h], 16) for h in range(8)], axis=0) for r in range(N)])}
def setup_inputs(rng):
    return dict({"x": rng.standard_normal((N, 128, T), dtype=np.float32).astype(ml_dtypes.bfloat16)}, **lists(rng, "uniform"))
def setup_inputs_comb(rng):
    d = setup_inputs(rng); d.update(lists(rng, "comb"))
    for k in ("x",): d[k] = (d[k].astype(np.float32) * 1048576.0).astype(d[k].dtype)
    return d
def setup_inputs_full(rng):
    d = setup_inputs(rng); d.update(lists(rng, "full"))
    for k in ("x",): d[k] = (d[k].astype(np.float32) * (1 / 1024.0)).astype(d[k].dtype)
    return d
def setup_inputs_none(rng):
    d = setup_inputs(rng); d.update(lists(rng, "none"))
    return d
def setup_inputs_one(rng):
    d = setup_inputs(rng); d.update(lists(rng, "one"))
    return d
def setup_inputs_run(rng):
    d = setup_inputs(rng); d.update(lists(rng, "run"))
    return d
def check_inputs(x):
    bad = []
    if x["keep"].min() < 0 or x["keep"].max() >= 2: bad.append("keep out of range")
    if max(int(a[16 * h:16 * h + 16].sum()) for a in x["keep"] for h in range(8)) > CAP: bad.append("a head keeps more than CAP columns on a rank")
    return bad
def reference(x, keep):
    y = np.zeros((128, N * CAP), x.dtype)
    for h in range(8):
        H = slice(16 * h, 16 * h + 16); got = np.concatenate([x[r][H][:, entries(keep[r][H]) > 0] for r in range(N)], axis=1); y[H, :got.shape[1]] = got
    return {"y": np.broadcast_to(y, (N, 128, N * CAP))}

@@ -1,0 +1,289 @@
+from concourse.bass import DstId, RemoteDMATransfer
+from concourse.mybir import AluOpType, ActivationFunctionType
+
+W = 256
+TX = 2048
+ZC = 2048
+
+SCRATCH = {
+    "kin": ("sbuf", [128, 128], "int32"),
+    "xin": ("sbuf", [128, TX + 16], "bfloat16"),
+    "kb": ("sbuf", [128, 128], "bfloat16"),
+    "run": ("sbuf", [128, 144], "bfloat16"),
+    "ones": ("sbuf", [128, 256], "bfloat16"),
+    "half": ("sbuf", [128, 128], "bfloat16"),
+    "blk": ("sbuf", [128, 128], "bfloat16"),
+    "tri": ("sbuf", [128, 128], "bfloat16"),
+    "eye": ("sbuf", [128, 128], "bfloat16"),
+    "zsel": ("sbuf", [128, 144], "bfloat16"),
+    "j3": ("sbuf", [128, 16, 16], "bfloat16"),
+    "j2": ("sbuf", [128, 256], "bfloat16"),
+    "colc": ("sbuf", [128, 8], "bfloat16"),
+    "cge": ("sbuf", [128, 16, 128], "bfloat16"),
+    "ptab": ("sbuf", [128, 144], "bfloat16"),
+    "offa": ("sbuf", [128, 8], "uint16"),
+    "offb": ("sbuf", [128, 8], "uint16"),
+    "cbf": ("sbuf", [128, 16], "bfloat16"),
+    "ile": ("sbuf", [128, 256], "bfloat16"),
+    "lst": ("sbuf", [128, 16], "uint16"),
+    "land": ("sbuf", [128, 8 * W + 16], "bfloat16"),
+    "cnt": ("sbuf", [128, 16], "float32"),
+    "nr": ("sbuf", [128, 8], "float32"),
+    "ends": ("sbuf", [128, 8], "float32"),
+    "step": ("sbuf", [128, 8], "float32"),
+    "dlt": ("sbuf", [128, 8], "float32"),
+    "one8": ("sbuf", [128, 8], "float32"),
+    "pcol": ("sbuf", [128, 8], "int32"),
+    "pmod": ("sbuf", [128, 8], "int32"),
+    "pmf": ("sbuf", [128, 8], "float32"),
+    "jb": ("sbuf", [128, 128], "float32"),
+    "jw": ("sbuf", [128, 128], "float32"),
+    "term": ("sbuf", [128, 1024], "float32"),
+    "sum4": ("sbuf", [128, 512], "float32"),
+    "sum2": ("sbuf", [128, 256], "float32"),
+    "sum1": ("sbuf", [128, 128], "float32"),
+    "offf": ("sbuf", [128, 128], "float32"),
+    "fin": ("sbuf", [128, 128], "uint16"),
+    "yb": ("sbuf", [128, TX], "bfloat16"),
+    "pcs": ("psum", [128, 512], "float32"),
+    "pcn": ("psum", [128, 512], "float32"),
+    "pps": ("psum", [128, 512], "float32"),
+    "pca": ("psum", [128, 512], "float32"),
+    "pcb": ("psum", [128, 512], "float32"),
+    "pis": ("psum", [128, 512], "float32"),
+}
+SEMAPHORES = ["ldk", "ldx", "cst", "c1", "gh", "gblk", "gtri", "gj", "geye", "gjw", "zs",
+              "v1", "v2", "v3", "v4", "v5", "v6", "v6b", "v7", "v9", "vj2", "vp1", "vp2", "vp3",
+              "p1", "p2", "p3", "p4", "p5", "p6", "s1", "s2", "s3", "pk", "pks",
+              "cpeer", "cpart", "dpeer", "down", "dpart", "lc", "ld",
+              "f1", "f2", "f3", "f4", "f5", "f6", "f7", "f8", "f9",
+              "y1", "y2", "y3", "y4", "st"]
+
+
+def rank_program(g, core, T, topo):
+    rank = T.rank_of(core)
+    if rank is None:
+        return
+    A = AluOpType
+    COPY = ActivationFunctionType.Copy
+    sem = T.sem
+    v, s, t = g.vector, g.scalar, g.tensor
+
+    cores = list(T.cores)
+
+    def rack_of(c):
+        return topo.rack(topo.host(c))
+
+    def rack_members(c):
+        return [d for d in cores if rack_of(d) == rack_of(c)]
+
+    def partner_of(c):
+        return [d for d in cores if rack_of(d) != rack_of(c) and topo.chip(d) == topo.chip(c) and topo.may_write(c, d)][0]
+
+    def slots_of(c):
+        m = rack_members(c)
+        return [m[m.index(c) ^ k] for k in range(4)]
+
+    partner = partner_of(core)
+    mine = slots_of(core)
+    order = mine + slots_of(partner)
+    slot = [order.index(c) for c in cores]
+
+    def ccol(k):
+        return 0 if k == 0 else 3 + k if k < 4 else 8 if k == 4 else 7 + k
+
+    def dst(d):
+        rid, pid = topo.addr(d, core)
+        return DstId(rid=rid, pnc=pid)
+
+    def fan(src, outs, arrive, left):
+        m = topo.mask(core, mine[1])
+        for d in mine[2:]:
+            m &= topo.mask(core, d)
+        g.remote_dma_fused([RemoteDMATransfer(dst_ids=[dst(d) for d in mine[1:]], dma_engine_mask=m, remote_sem=arrive,
+                                              srcs=[src], dsts=outs)], local_sem=left)
+        return bin(m).count("1")
+
+    def across(out, src, arrive, left):
+        rid, pid = topo.addr(partner, core)
+        m = topo.mask(core, partner)
+        g.remote_dma(out, src, arrive, left, pid, rid, m)
+        return bin(m).count("1")
+
+    g.sync.dma_start(T.kin[:], T.keep[:]).then_inc(sem.ldk, 16)
+    g.sync.dma_start(T.xin[:, 0:TX], T.x[:]).then_inc(sem.ldx, 16)
+
+    v.memset(T.ones[:], 1.0).then_inc(sem.c1, 1)
+    v.memset(T.run[:, 0:1], 0.0).then_inc(sem.cst, 1)
+    v.memset(T.zsel[:], 0.0).then_inc(sem.cst, 1)
+    v.memset(T.ptab[:, 128:144], 1024.0).then_inc(sem.cst, 1)
+    v.memset(T.cnt[:, 0:4], 0.0).then_inc(sem.cst, 1)
+    v.memset(T.xin[:, TX:TX + 16], 0.0).then_inc(sem.cst, 1)
+    v.memset(T.land[:, 8 * W:8 * W + 16], 0.0).then_inc(sem.cst, 1)
+    NCST = 6
+    v.wait_ge(sem.c1, 1)
+    v.tensor_tensor_scan(T.j2[:], T.ones[:], T.ones[:], -1.0, A.mult, A.add).then_inc(sem.vj2, 1)
+    v.wait_ge(sem.cst, NCST)
+
+    g.wait_ge(sem.c1, 1)
+    g.affine_select(T.half[:], T.ones[:, 0:128], [[-16, 8], [0, 16]], A.is_ge, 0.0, 0, 1).then_inc(sem.gh, 1)
+    g.wait_ge(sem.gh, 1)
+    g.affine_select(T.blk[:], T.half[:], [[16, 8], [0, 16]], A.is_ge, 0.0, 15, -1).then_inc(sem.gblk, 1)
+    g.iota(T.j3[:], [[16, 16], [1, 16]], 0, 0, allow_small_or_imprecise_dtypes=True).then_inc(sem.gj, 1)
+    g.wait_ge(sem.gblk, 1)
+    g.affine_select(T.tri[:], T.blk[:], [[1, 128]], A.is_ge, 0.0, 0, -1).then_inc(sem.gtri, 1)
+    g.affine_select(T.eye[:], T.ones[:, 0:128], [[1, 128]], A.is_equal, 0.0, 0, -1).then_inc(sem.geye, 1)
+
+    v.wait_ge(sem.gblk, 1)
+    v.tensor_copy(T.zsel[:, 15:143:16], T.blk[:, 0:128:16]).then_inc(sem.zs, 1)
+
+    v.wait_ge(sem.ldk, 16)
+    v.tensor_copy(T.kb[:], T.kin[:]).then_inc(sem.v1, 1)
+    v.wait_ge(sem.v1, 1)
+    v.tensor_tensor_scan(T.run[:, 1:129], T.ones[:, 0:128], T.kb[:], 0.0, A.mult, A.add).then_inc(sem.v2, 1)
+
+    t.wait_ge(sem.gblk, 1)
+    t.wait_ge(sem.cst, NCST)
+    t.wait_ge(sem.v1, 1)
+    t.wait_ge(sem.v2, 1)
+    t.matmul(T.pcs[:, 0:8], T.run[:, 1:129], T.blk[:, 0:128:16], True, True).then_inc(sem.p1, 1)
+    t.matmul(T.pcn[:, 0:1], T.blk[:], T.run[:, 128:129], True, True).then_inc(sem.p2, 1)
+    t.matmul(T.pps[:, 0:128], T.blk[:], T.run[:, 0:128], True, False)
+    t.wait_ge(sem.gtri, 1)
+    t.matmul(T.pps[:, 0:128], T.tri[:], T.kb[:], False, True).then_inc(sem.p3, 1)
+
+    s.wait_ge(sem.cst, NCST)
+    s.wait_ge(sem.p2, 1)
+    s.activation(T.cnt[:, 0:1], T.pcn[:, 0:1], COPY).then_inc(sem.s1, 1)
+    s.wait_ge(sem.p3, 1)
+    s.activation(T.ptab[:, 0:128], T.pps[:, 0:128], COPY).then_inc(sem.s2, 1)
+
+    v.wait_ge(sem.p1, 1)
+    v.tensor_copy(T.colc[:], T.pcs[:, 0:8]).then_inc(sem.v3, 1)
+    v.wait_ge(sem.gj, 1)
+    v.wait_ge(sem.v3, 1)
+    for lo, done in ((0, sem.v4), (8, sem.v5)):
+        for h in range(8):
+            v.tensor_scalar(T.cge[:, lo:lo + 8, 16 * h:16 * h + 16], T.j3[:, lo:lo + 8, :], T.colc[:, h:h + 1], None,
+                            A.is_ge).then_inc(done, 1)
+    for lo, ready, out, done in ((0, sem.v4, T.pca, sem.p4), (8, sem.v5, T.pcb, sem.p5)):
+        t.wait_ge(ready, 8)
+        for b in range(8):
+            t.matmul(out[:, b:b + 1], T.cge[:, lo + b, :], T.ones[:, 0:1], True, True).then_inc(done, 1)
+
+    v.wait_ge(sem.p4, 8)
+    v.tensor_copy(T.offa[:], T.pca[:, 0:8]).then_inc(sem.v6, 1)
+    v.wait_ge(sem.v6, 1)
+    v.wait_ge(sem.vj2, 1)
+    v.wait_ge(sem.s2, 1)
+    v.tensor_tensor(T.ile[:, 0:128], T.ptab[:, 0:129].indirect(T.offa[:, 0:8]), T.j2[:, 0:128], A.is_le).then_inc(sem.v7, 1)
+    v.wait_ge(sem.p5, 8)
+    v.tensor_copy(T.offb[:], T.pcb[:, 0:8]).then_inc(sem.v6b, 1)
+    v.wait_ge(sem.v6b, 1)
+    v.tensor_tensor(T.ile[:, 128:256], T.ptab[:, 0:129].indirect(T.offb[:, 0:8]), T.j2[:, 128:256],
+                    A.is_le).then_inc(sem.v7, 1)
+
+    s.wait_ge(sem.v6, 1)
+    s.activation(T.cbf[:, 0:8], T.pca[:, 0:8], COPY, scale=16.0).then_inc(sem.s3, 1)
+    s.wait_ge(sem.v6b, 1)
+    s.activation(T.cbf[:, 8:16], T.pcb[:, 0:8], COPY, scale=16.0).then_inc(sem.s3, 1)
+
+    t.wait_ge(sem.geye, 1)
+    t.wait_ge(sem.zs, 1)
+    t.wait_ge(sem.s3, 2)
+    t.matmul(T.pis[:, 0:16], T.eye[:], T.cbf[:], True, False)
+    t.wait_ge(sem.v7, 2)
+    for a in range(16):
+        mm = t.matmul(T.pis[:, 0:16], T.zsel[:, 15 - a:143 - a], T.ile[:, a:256:16], False, a == 15)
+        if a == 15:
+            mm.then_inc(sem.p6, 1)
+
+    v.wait_ge(sem.p6, 1)
+    v.tensor_copy(T.lst[:], T.pis[:, 0:16]).then_inc(sem.v9, 1)
+    v.wait_ge(sem.v9, 1)
+    v.wait_ge(sem.ldx, 16)
+    v.tensor_copy(T.land[:, 0:128], T.xin[:].indirect(T.lst[:, 0:8])).then_inc(sem.pk, 1)
+    s.wait_ge(sem.v9, 1)
+    s.wait_ge(sem.ldx, 16)
+    s.activation(T.land[:, 128:256], T.xin[:].indirect(T.lst[:, 8:16]), COPY).then_inc(sem.pks, 1)
+
+    g.wait_ge(sem.s1, 1)
+    ne = fan(T.cnt[:, 0:1], [T.cnt[:, ccol(k):ccol(k) + 1] for k in (1, 2, 3)], sem.cpeer, sem.lc)
+    nlc = ne
+    g.iota(T.pcol[:], [[0, 8]], 0, 1).then_inc(sem.gjw, 1)
+    g.iota(T.jb[:], [[16, 128]], 0, 0, allow_small_or_imprecise_dtypes=True).then_inc(sem.gjw, 1)
+    g.wait_ge(sem.pk, 1)
+    g.wait_ge(sem.pks, 1)
+    nld = fan(T.land[:, 0:W], [T.land[:, k * W:(k + 1) * W] for k in (1, 2, 3)], sem.dpeer, sem.ld)
+    nx = across(T.land[:, 4 * W:5 * W], T.land[:, 0:W], sem.down, sem.ld)
+    nld += nx
+    g.wait_ge(sem.cpeer, 3 * ne)
+    nlc += across(T.cnt[:, 8:15], T.cnt[:, 0:7], sem.cpart, sem.lc) if False else 0
+    nlc += _counts_across(T, across, sem)
+    g.wait_ge(sem.dpeer, 3 * ne)
+    nld += across(T.land[:, 5 * W:8 * W], T.land[:, W:4 * W], sem.dpart, sem.ld)
+    g.wait_ge(sem.lc, nlc)
+    g.wait_ge(sem.ld, nld)
+
+    v.wait_ge(sem.gjw, 2)
+    v.tensor_scalar(T.pmod[:], T.pcol[:], 15, None, A.bitwise_and).then_inc(sem.vp1, 1)
+    v.wait_ge(sem.vp1, 1)
+    v.tensor_copy(T.pmf[:], T.pmod[:]).then_inc(sem.vp2, 1)
+    v.wait_ge(sem.vp2, 1)
+    v.tensor_scalar(T.jw[:], T.jb[:], T.pmf[:, 0:1], float(W * slot[0]), A.add, A.add).then_inc(sem.vp3, 1)
+    v.tensor_scalar(T.offf[:], T.jb[:], T.pmf[:, 0:1], None, A.add).then_inc(sem.vp3, 1)
+    v.memset(T.one8[:], 1.0).then_inc(sem.f1, 1)
+    for r in range(8):
+        d = float(W * (slot[r + 1] - slot[r])) if r < 7 else 8192.0
+        v.memset(T.step[:, r:r + 1], d).then_inc(sem.f1, 1)
+    v.wait_ge(sem.f1, 9)
+    v.wait_ge(sem.s1, 1)
+    v.wait_ge(sem.cpeer, 3 * ne)
+    v.wait_ge(sem.cpart, nx)
+    for r in range(8):
+        c = ccol(slot[r])
+        v.tensor_copy(T.nr[:, r:r + 1], T.cnt[:, c:c + 1]).then_inc(sem.f2, 1)
+    v.wait_ge(sem.f2, 8)
+    v.tensor_tensor_scan(T.ends[:], T.one8[:], T.nr[:], 0.0, A.mult, A.add).then_inc(sem.f3, 1)
+    v.tensor_tensor(T.dlt[:], T.step[:], T.nr[:], A.subtract).then_inc(sem.f3, 1)
+    v.wait_ge(sem.f3, 2)
+    v.wait_ge(sem.vp3, 2)
+    for r in range(8):
+        v.tensor_scalar(T.term[:, 128 * r:128 * r + 128], T.offf[:], T.ends[:, r:r + 1], T.dlt[:, r:r + 1],
+                        A.is_ge, A.mult).then_inc(sem.f4, 1)
+    v.wait_ge(sem.f4, 8)
+    v.tensor_tensor(T.sum4[:], T.term[:, 0:512], T.term[:, 512:1024], A.add).then_inc(sem.f5, 1)
+    v.wait_ge(sem.f5, 1)
+    v.tensor_tensor(T.sum2[:], T.sum4[:, 0:256], T.sum4[:, 256:512], A.add).then_inc(sem.f6, 1)
+    v.wait_ge(sem.f6, 1)
+    v.tensor_tensor(T.sum1[:], T.sum2[:, 0:128], T.sum2[:, 128:256], A.add).then_inc(sem.f7, 1)
+    v.wait_ge(sem.f7, 1)
+    v.tensor_tensor(T.term[:, 0:128], T.sum1[:], T.jw[:], A.add).then_inc(sem.f8, 1)
+    v.wait_ge(sem.f8, 1)
+    v.tensor_scalar(T.fin[:], T.term[:, 0:128], float(ZC), None, A.min).then_inc(sem.f9, 1)
+
+    for q in (v, s):
+        q.wait_ge(sem.f9, 1)
+        q.wait_ge(sem.pk, 1)
+        q.wait_ge(sem.pks, 1)
+        q.wait_ge(sem.dpeer, 3 * ne)
+        q.wait_ge(sem.down, nx)
+        q.wait_ge(sem.dpart, nx)
+    H = TX // 4
+    win = T.land[:]
+    for n in (0, 1):
+        v.tensor_copy(T.yb[:, n * H:(n + 1) * H],
+                      win.indirect(T.fin[:, n * H // 16:(n + 1) * H // 16])).then_inc((sem.y1, sem.y2)[n], 1)
+        m = n + 2
+        s.activation(T.yb[:, m * H:(m + 1) * H], win.indirect(T.fin[:, m * H // 16:(m + 1) * H // 16]),
+                     COPY).then_inc((sem.y3, sem.y4)[n], 1)
+    for m, done in ((0, sem.y1), (2, sem.y3), (1, sem.y2)):
+        g.sync.wait_ge(done, 1)
+        g.sync.dma_start(T.y[:, m * H:(m + 1) * H], T.yb[:, m * H:(m + 1) * H]).then_inc(sem.st, 16)
+    s.wait_ge(sem.y4, 1)
+    s.dma_start(T.y[:, 3 * H:4 * H], T.yb[:, 3 * H:4 * H]).then_inc(sem.st, 16)
+    g.sync.wait_ge(sem.st, 64)
+
+
+def _counts_across(T, across, sem):
+    return across(T.cnt[:, 8:15], T.cnt[:, 0:7], sem.cpart, sem.lc)

@@ -55,7 +55,7 @@ SCRATCH = {
 SEMAPHORES = ["ldk", "ldx", "cst", "c1", "gh", "gblk", "gtri", "gj", "geye", "gjw", "zs",
               "v1", "v2", "v3", "v4", "v5", "v6", "v6b", "v7", "v9", "vj2", "vp1", "vp2", "vp3",
               "p1", "p2", "p3", "p4", "p5", "p6", "s1", "s2", "s3", "pk", "pks",
-              "cpeer", "cpart", "dpeer", "down", "dpart", "lc", "ld",
+              "cpeer", "cpart", "dpeer", "down", "drel", "lc", "ld",
               "f1", "f2", "f3", "f4", "f5", "f6", "f7", "f8", "f9",
               "y1", "y2", "y3", "y4", "st"]
 
@@ -80,27 +80,33 @@ def rank_program(g, core, T, topo):
     def partner_of(c):
         return [d for d in cores if rack_of(d) != rack_of(c) and topo.chip(d) == topo.chip(c) and topo.may_write(c, d)][0]
 
-    def slots_of(c):
+    def rack_slots(c):
         m = rack_members(c)
         return [m[m.index(c) ^ k] for k in range(4)]
 
+    def slots_of(c):
+        return rack_slots(c) + rack_slots(partner_of(c))
+
     partner = partner_of(core)
-    mine = slots_of(core)
-    order = mine + slots_of(partner)
+    order = slots_of(core)
+    peers = order[1:4]
     slot = [order.index(c) for c in cores]
 
     def ccol(k):
         return 0 if k == 0 else 3 + k if k < 4 else 8 if k == 4 else 7 + k
+
+    def land(k):
+        return T.land[:, k * W:(k + 1) * W]
 
     def dst(d):
         rid, pid = topo.addr(d, core)
         return DstId(rid=rid, pnc=pid)
 
     def fan(src, outs, arrive, left):
-        m = topo.mask(core, mine[1])
-        for d in mine[2:]:
+        m = topo.mask(core, peers[0])
+        for d in peers[1:]:
             m &= topo.mask(core, d)
-        g.remote_dma_fused([RemoteDMATransfer(dst_ids=[dst(d) for d in mine[1:]], dma_engine_mask=m, remote_sem=arrive,
+        g.remote_dma_fused([RemoteDMATransfer(dst_ids=[dst(d) for d in peers], dma_engine_mask=m, remote_sem=arrive,
                                               srcs=[src], dsts=outs)], local_sem=left)
         return bin(m).count("1")
 
@@ -214,14 +220,12 @@ def rank_program(g, core, T, topo):
     g.iota(T.jb[:], [[16, 128]], 0, 0, allow_small_or_imprecise_dtypes=True).then_inc(sem.gjw, 1)
     g.wait_ge(sem.pk, 1)
     g.wait_ge(sem.pks, 1)
-    nld = fan(T.land[:, 0:W], [T.land[:, k * W:(k + 1) * W] for k in (1, 2, 3)], sem.dpeer, sem.ld)
-    nx = across(T.land[:, 4 * W:5 * W], T.land[:, 0:W], sem.down, sem.ld)
-    nld += nx
+    nx = across(land(4), land(0), sem.down, sem.ld)
+    nld = nx + fan(land(0), [land(slots_of(d).index(core)) for d in peers], sem.dpeer, sem.ld)
     g.wait_ge(sem.cpeer, 3 * ne)
-    nlc += across(T.cnt[:, 8:15], T.cnt[:, 0:7], sem.cpart, sem.lc) if False else 0
-    nlc += _counts_across(T, across, sem)
-    g.wait_ge(sem.dpeer, 3 * ne)
-    nld += across(T.land[:, 5 * W:8 * W], T.land[:, W:4 * W], sem.dpart, sem.ld)
+    nlc += across(T.cnt[:, 8:15], T.cnt[:, 0:7], sem.cpart, sem.lc)
+    g.wait_ge(sem.down, nx)
+    nld += fan(land(4), [land(slots_of(d).index(partner)) for d in peers], sem.drel, sem.ld)
     g.wait_ge(sem.lc, nlc)
     g.wait_ge(sem.ld, nld)
 
@@ -268,7 +272,7 @@ def rank_program(g, core, T, topo):
         q.wait_ge(sem.pks, 1)
         q.wait_ge(sem.dpeer, 3 * ne)
         q.wait_ge(sem.down, nx)
-        q.wait_ge(sem.dpart, nx)
+        q.wait_ge(sem.drel, 3 * ne)
     H = TX // 4
     win = T.land[:]
     for n in (0, 1):
@@ -283,7 +287,3 @@ def rank_program(g, core, T, topo):
     s.wait_ge(sem.y4, 1)
     s.dma_start(T.y[:, 3 * H:4 * H], T.yb[:, 3 * H:4 * H]).then_inc(sem.st, 16)
     g.sync.wait_ge(sem.st, 64)
-
-
-def _counts_across(T, across, sem):
-    return across(T.cnt[:, 8:15], T.cnt[:, 0:7], sem.cpart, sem.lc)

@@ -2,8 +2,10 @@ from concourse.bass import DstId, RemoteDMATransfer
 from concourse.mybir import AluOpType, ActivationFunctionType
 
 W = 256
+HW = W // 2
 TX = 2048
 ZC = 2048
+WORLD = 512
 
 SCRATCH = {
     "kin": ("sbuf", [128, 128], "int32"),
@@ -27,8 +29,8 @@ SCRATCH = {
     "ile": ("sbuf", [128, 256], "bfloat16"),
     "lst": ("sbuf", [128, 16], "uint16"),
     "land": ("sbuf", [128, 8 * W + 16], "bfloat16"),
-    "cnt": ("sbuf", [128, 16], "float32"),
-    "nr": ("sbuf", [128, 8], "float32"),
+    "cown": ("sbuf", [128, 8], "float32"),
+    "cnt": ("sbuf", [128, 8], "float32"),
     "ends": ("sbuf", [128, 8], "float32"),
     "step": ("sbuf", [128, 8], "float32"),
     "dlt": ("sbuf", [128, 8], "float32"),
@@ -54,22 +56,22 @@ SCRATCH = {
 }
 SEMAPHORES = ["ldk", "ldx", "cst", "c1", "gh", "gblk", "gtri", "gj", "geye", "gjw", "zs",
               "v1", "v2", "v3", "v4", "v5", "v6", "v6b", "v7", "v9", "vj2", "vp1", "vp2", "vp3",
-              "p1", "p2", "p3", "p4", "p5", "p6", "s1", "s2", "s3", "pk", "pks",
-              "cpeer", "cpart", "dpeer", "down", "drel", "lc", "ld",
+              "p1", "p2", "p3", "p4", "p5", "p6", "s1", "s2", "s3", "pk", "pk2",
+              "cpeer", "cpart", "dpeer", "down", "down2", "drel", "lc", "ld",
               "f1", "f2", "f3", "f4", "f5", "f6", "f7", "f8", "f9",
               "y1", "y2", "y3", "y4", "st"]
 
 
 def rank_program(g, core, T, topo):
-    rank = T.rank_of(core)
-    if rank is None:
-        return
     A = AluOpType
     COPY = ActivationFunctionType.Copy
     sem = T.sem
     v, s, t = g.vector, g.scalar, g.tensor
 
     cores = list(T.cores)
+
+    def same_chip(a, b):
+        return topo.host(a) == topo.host(b) and topo.chip(a) == topo.chip(b)
 
     def rack_of(c):
         return topo.rack(topo.host(c))
@@ -87,28 +89,37 @@ def rank_program(g, core, T, topo):
     def slots_of(c):
         return rack_slots(c) + rack_slots(partner_of(c))
 
+    def helper_of(c):
+        return [d for d in range(WORLD) if same_chip(c, d) and topo.die(d) != topo.die(c)
+                and all(topo.may_write(d, e) for e in rack_members(c))][0]
+
+    def fan(src, dests, outs, arrive, left):
+        m = topo.mask(core, dests[0])
+        for d in dests[1:]:
+            m &= topo.mask(core, d)
+        ids = [topo.addr(d, core) for d in dests]
+        g.remote_dma_fused([RemoteDMATransfer(dst_ids=[DstId(rid=rid, pnc=pid) for rid, pid in ids], dma_engine_mask=m,
+                                              remote_sem=arrive, srcs=[src], dsts=outs)], local_sem=left)
+        return bin(m).count("1")
+
+    rank = T.rank_of(core)
+    if rank is None:
+        for d in cores:
+            if same_chip(core, d) and core == helper_of(d):
+                far = partner_of(d)
+                r = cores.index(far)
+                g.wait_ge(sem.cpeer, bin(topo.mask(far, core)).count("1"))
+                members = rack_slots(d)[1:] + [d]
+                g.wait_ge(sem.lc, fan(T.cnt[:, r:r + 1], members, [T.cnt[:, r:r + 1]] * 4, sem.cpart, sem.lc))
+        return
+
     partner = partner_of(core)
     order = slots_of(core)
     peers = order[1:4]
     slot = [order.index(c) for c in cores]
 
-    def ccol(k):
-        return 0 if k == 0 else 3 + k if k < 4 else 8 if k == 4 else 7 + k
-
-    def land(k):
-        return T.land[:, k * W:(k + 1) * W]
-
-    def dst(d):
-        rid, pid = topo.addr(d, core)
-        return DstId(rid=rid, pnc=pid)
-
-    def fan(src, outs, arrive, left):
-        m = topo.mask(core, peers[0])
-        for d in peers[1:]:
-            m &= topo.mask(core, d)
-        g.remote_dma_fused([RemoteDMATransfer(dst_ids=[dst(d) for d in peers], dma_engine_mask=m, remote_sem=arrive,
-                                              srcs=[src], dsts=outs)], local_sem=left)
-        return bin(m).count("1")
+    def land(k, lo=0, hi=W):
+        return T.land[:, k * W + lo:k * W + hi]
 
     def across(out, src, arrive, left):
         rid, pid = topo.addr(partner, core)
@@ -123,10 +134,9 @@ def rank_program(g, core, T, topo):
     v.memset(T.run[:, 0:1], 0.0).then_inc(sem.cst, 1)
     v.memset(T.zsel[:], 0.0).then_inc(sem.cst, 1)
     v.memset(T.ptab[:, 128:144], 1024.0).then_inc(sem.cst, 1)
-    v.memset(T.cnt[:, 0:4], 0.0).then_inc(sem.cst, 1)
     v.memset(T.xin[:, TX:TX + 16], 0.0).then_inc(sem.cst, 1)
     v.memset(T.land[:, 8 * W:8 * W + 16], 0.0).then_inc(sem.cst, 1)
-    NCST = 6
+    NCST = 5
     v.wait_ge(sem.c1, 1)
     v.tensor_tensor_scan(T.j2[:], T.ones[:], T.ones[:], -1.0, A.mult, A.add).then_inc(sem.vj2, 1)
     v.wait_ge(sem.cst, NCST)
@@ -158,9 +168,9 @@ def rank_program(g, core, T, topo):
     t.wait_ge(sem.gtri, 1)
     t.matmul(T.pps[:, 0:128], T.tri[:], T.kb[:], False, True).then_inc(sem.p3, 1)
 
-    s.wait_ge(sem.cst, NCST)
     s.wait_ge(sem.p2, 1)
-    s.activation(T.cnt[:, 0:1], T.pcn[:, 0:1], COPY).then_inc(sem.s1, 1)
+    s.activation(T.cown[:, 0:1], T.pcn[:, 0:1], COPY).then_inc(sem.s1, 1)
+    s.wait_ge(sem.cst, NCST)
     s.wait_ge(sem.p3, 1)
     s.activation(T.ptab[:, 0:128], T.pps[:, 0:128], COPY).then_inc(sem.s2, 1)
 
@@ -206,27 +216,29 @@ def rank_program(g, core, T, topo):
 
     v.wait_ge(sem.p6, 1)
     v.tensor_copy(T.lst[:], T.pis[:, 0:16]).then_inc(sem.v9, 1)
-    v.wait_ge(sem.v9, 1)
-    v.wait_ge(sem.ldx, 16)
-    v.tensor_copy(T.land[:, 0:128], T.xin[:].indirect(T.lst[:, 0:8])).then_inc(sem.pk, 1)
-    s.wait_ge(sem.v9, 1)
-    s.wait_ge(sem.ldx, 16)
-    s.activation(T.land[:, 128:256], T.xin[:].indirect(T.lst[:, 8:16]), COPY).then_inc(sem.pks, 1)
+    Q = W // 4
+    for q in (v, s):
+        q.wait_ge(sem.v9, 1)
+        q.wait_ge(sem.ldx, 16)
+    for lo, done in ((0, sem.pk), (HW, sem.pk2)):
+        v.tensor_copy(land(0, lo, lo + Q), T.xin[:].indirect(T.lst[:, lo // 16:(lo + Q) // 16])).then_inc(done, 1)
+        s.activation(land(0, lo + Q, lo + HW), T.xin[:].indirect(T.lst[:, (lo + Q) // 16:(lo + HW) // 16]),
+                     COPY).then_inc(done, 1)
 
     g.wait_ge(sem.s1, 1)
-    ne = fan(T.cnt[:, 0:1], [T.cnt[:, ccol(k):ccol(k) + 1] for k in (1, 2, 3)], sem.cpeer, sem.lc)
-    nlc = ne
+    ne = fan(T.cown[:, 0:1], peers + [helper_of(partner)], [T.cnt[:, rank:rank + 1]] * 4, sem.cpeer, sem.lc)
     g.iota(T.pcol[:], [[0, 8]], 0, 1).then_inc(sem.gjw, 1)
     g.iota(T.jb[:], [[16, 128]], 0, 0, allow_small_or_imprecise_dtypes=True).then_inc(sem.gjw, 1)
-    g.wait_ge(sem.pk, 1)
-    g.wait_ge(sem.pks, 1)
-    nx = across(land(4), land(0), sem.down, sem.ld)
-    nld = nx + fan(land(0), [land(slots_of(d).index(core)) for d in peers], sem.dpeer, sem.ld)
-    g.wait_ge(sem.cpeer, 3 * ne)
-    nlc += across(T.cnt[:, 8:15], T.cnt[:, 0:7], sem.cpart, sem.lc)
-    g.wait_ge(sem.down, nx)
-    nld += fan(land(4), [land(slots_of(d).index(partner)) for d in peers], sem.drel, sem.ld)
-    g.wait_ge(sem.lc, nlc)
+    g.wait_ge(sem.pk, 2)
+    nx = across(land(4, 0, HW), land(0, 0, HW), sem.down, sem.ld)
+    g.wait_ge(sem.pk2, 2)
+    nld = nx + across(land(4, HW, W), land(0, HW, W), sem.down2, sem.ld)
+    nld += fan(land(0), peers, [land(slots_of(d).index(core)) for d in peers], sem.dpeer, sem.ld)
+    for lo, arrived in ((0, sem.down), (HW, sem.down2)):
+        g.wait_ge(arrived, nx)
+        nld += fan(land(4, lo, lo + HW), peers, [land(slots_of(d).index(partner), lo, lo + HW) for d in peers],
+                   sem.drel, sem.ld)
+    g.wait_ge(sem.lc, ne)
     g.wait_ge(sem.ld, nld)
 
     v.wait_ge(sem.gjw, 2)
@@ -243,13 +255,11 @@ def rank_program(g, core, T, topo):
     v.wait_ge(sem.f1, 9)
     v.wait_ge(sem.s1, 1)
     v.wait_ge(sem.cpeer, 3 * ne)
-    v.wait_ge(sem.cpart, nx)
-    for r in range(8):
-        c = ccol(slot[r])
-        v.tensor_copy(T.nr[:, r:r + 1], T.cnt[:, c:c + 1]).then_inc(sem.f2, 1)
-    v.wait_ge(sem.f2, 8)
-    v.tensor_tensor_scan(T.ends[:], T.one8[:], T.nr[:], 0.0, A.mult, A.add).then_inc(sem.f3, 1)
-    v.tensor_tensor(T.dlt[:], T.step[:], T.nr[:], A.subtract).then_inc(sem.f3, 1)
+    v.wait_ge(sem.cpart, 4 * ne)
+    v.tensor_copy(T.cnt[:, rank:rank + 1], T.cown[:, 0:1]).then_inc(sem.f2, 1)
+    v.wait_ge(sem.f2, 1)
+    v.tensor_tensor_scan(T.ends[:], T.one8[:], T.cnt[:], 0.0, A.mult, A.add).then_inc(sem.f3, 1)
+    v.tensor_tensor(T.dlt[:], T.step[:], T.cnt[:], A.subtract).then_inc(sem.f3, 1)
     v.wait_ge(sem.f3, 2)
     v.wait_ge(sem.vp3, 2)
     for r in range(8):
@@ -268,11 +278,12 @@ def rank_program(g, core, T, topo):
 
     for q in (v, s):
         q.wait_ge(sem.f9, 1)
-        q.wait_ge(sem.pk, 1)
-        q.wait_ge(sem.pks, 1)
+        q.wait_ge(sem.pk, 2)
+        q.wait_ge(sem.pk2, 2)
         q.wait_ge(sem.dpeer, 3 * ne)
         q.wait_ge(sem.down, nx)
-        q.wait_ge(sem.drel, 3 * ne)
+        q.wait_ge(sem.down2, nx)
+        q.wait_ge(sem.drel, 6 * ne)
     H = TX // 4
     win = T.land[:]
     for n in (0, 1):

@@ -6,60 +6,32 @@ HW = W // 2
 TX = 2048
 ZC = 2048
 WORLD = 512
+PIECES = (288, 448, 288)
+
+
+def _sb(cols, kind="bfloat16"):
+    return ("sbuf", [128] + cols, kind)
+
 
 SCRATCH = {
-    "kin": ("sbuf", [128, 128], "int32"),
-    "xin": ("sbuf", [128, TX + 16], "bfloat16"),
-    "kb": ("sbuf", [128, 128], "bfloat16"),
-    "run": ("sbuf", [128, 144], "bfloat16"),
-    "ones": ("sbuf", [128, 256], "bfloat16"),
-    "half": ("sbuf", [128, 128], "bfloat16"),
-    "blk": ("sbuf", [128, 128], "bfloat16"),
-    "tri": ("sbuf", [128, 128], "bfloat16"),
-    "eye": ("sbuf", [128, 128], "bfloat16"),
-    "zsel": ("sbuf", [128, 144], "bfloat16"),
-    "j3": ("sbuf", [128, 16, 16], "bfloat16"),
-    "j2": ("sbuf", [128, 256], "bfloat16"),
-    "colc": ("sbuf", [128, 8], "bfloat16"),
-    "cge": ("sbuf", [128, 16, 128], "bfloat16"),
-    "ptab": ("sbuf", [128, 144], "bfloat16"),
-    "offa": ("sbuf", [128, 8], "uint16"),
-    "offb": ("sbuf", [128, 8], "uint16"),
-    "cbf": ("sbuf", [128, 16], "bfloat16"),
-    "ile": ("sbuf", [128, 256], "bfloat16"),
-    "lst": ("sbuf", [128, 16], "uint16"),
-    "land": ("sbuf", [128, 8 * W + 16], "bfloat16"),
-    "cown": ("sbuf", [128, 8], "float32"),
-    "cnt": ("sbuf", [128, 8], "float32"),
-    "ends": ("sbuf", [128, 8], "float32"),
-    "step": ("sbuf", [128, 8], "float32"),
-    "dlt": ("sbuf", [128, 8], "float32"),
-    "one8": ("sbuf", [128, 8], "float32"),
-    "pcol": ("sbuf", [128, 8], "int32"),
-    "pmod": ("sbuf", [128, 8], "int32"),
-    "pmf": ("sbuf", [128, 8], "float32"),
-    "jb": ("sbuf", [128, 128], "float32"),
-    "jw": ("sbuf", [128, 128], "float32"),
-    "term": ("sbuf", [128, 1024], "float32"),
-    "sum4": ("sbuf", [128, 512], "float32"),
-    "sum2": ("sbuf", [128, 256], "float32"),
-    "sum1": ("sbuf", [128, 128], "float32"),
-    "offf": ("sbuf", [128, 128], "float32"),
-    "fin": ("sbuf", [128, 128], "uint16"),
-    "yb": ("sbuf", [128, TX], "bfloat16"),
-    "pcs": ("psum", [128, 512], "float32"),
-    "pcn": ("psum", [128, 512], "float32"),
-    "pps": ("psum", [128, 512], "float32"),
-    "pca": ("psum", [128, 512], "float32"),
-    "pcb": ("psum", [128, 512], "float32"),
-    "pis": ("psum", [128, 512], "float32"),
+    "kin": _sb([128], "int32"), "xin": _sb([TX + 16]), "kb": _sb([128]), "run": _sb([144]),
+    "ones": _sb([256]), "inv": _sb([128]), "dz": _sb([128]), "dm": _sb([128]), "hq": _sb([128]), "m16": _sb([128]),
+    "r16": _sb([128]), "upto": _sb([8]), "ind": _sb([8]), "blk": _sb([128]), "tri": _sb([128]), "eye": _sb([128]),
+    "mb": _sb([128]), "j3": _sb([16, 16]), "j2": _sb([256]), "colc": _sb([8]), "cge": _sb([16, 128]),
+    "ptab": _sb([144]), "offa": _sb([8], "uint16"), "offb": _sb([8], "uint16"), "cbf": _sb([16]), "ile": _sb([256]),
+    "ym": _sb([256]), "lst": _sb([16], "uint16"), "land": _sb([8 * W + 16]), "cnt": _sb([32], "float32"),
+    "ju": _sb([128], "uint16"), "ends": _sb([8], "float32"), "dlt": _sb([8], "float32"), "one8": _sb([8], "float32"),
+    "term": _sb([1024]), "fin": _sb([128], "uint16"), "yb": _sb([TX]),
 }
-SEMAPHORES = ["ldk", "ldx", "cst", "c1", "gh", "gblk", "gtri", "gj", "geye", "gjw", "zs",
-              "v1", "v2", "v3", "v4", "v5", "v6", "v6b", "v7", "v9", "vj2", "vp1", "vp2", "vp3",
-              "p1", "p2", "p3", "p4", "p5", "p6", "s1", "s2", "s3", "pk", "pk2",
+for _k in range(8):
+    SCRATCH["b%d" % _k] = ("psum", [128, 512], "float32")
+SEMAPHORES = ["ldk", "ldx", "cst", "k0", "k1", "k2", "k3", "k4", "k5", "kp", "kr", "gup", "gind", "gj", "gblk", "gtri",
+              "geye", "gmb",
+              "v1", "v2", "v3", "v4", "v5", "v6", "v6b", "v7a", "v7b", "v8a", "v8b", "v9a", "v9b", "vj2",
+              "p1", "p2", "p3", "p4", "p5", "p6a", "p6b", "pya", "pyb", "pj", "pf", "s1", "s2", "s3a", "s3b", "pk", "pk2",
               "cpeer", "cpart", "dpeer", "down", "down2", "drel", "lc", "ld",
-              "f1", "f2", "f3", "f4", "f5", "f6", "f7", "f8", "f9",
-              "y1", "y2", "y3", "y4", "st"]
+              "f1", "f2", "f3", "f4", "f9",
+              "yv0", "yv1", "yv2", "ys0", "ys1", "ys2", "st"]
 
 
 def rank_program(g, core, T, topo):
@@ -76,31 +48,34 @@ def rank_program(g, core, T, topo):
     def rack_of(c):
         return topo.rack(topo.host(c))
 
-    def rack_members(c):
-        return [d for d in cores if rack_of(d) == rack_of(c)]
+    def peers_of(c):
+        m = [d for d in cores if rack_of(d) == rack_of(c)]
+        return [m[m.index(c) ^ k] for k in range(1, 4)]
 
     def partner_of(c):
         return [d for d in cores if rack_of(d) != rack_of(c) and topo.chip(d) == topo.chip(c) and topo.may_write(c, d)][0]
 
-    def rack_slots(c):
-        m = rack_members(c)
-        return [m[m.index(c) ^ k] for k in range(4)]
-
-    def slots_of(c):
-        return rack_slots(c) + rack_slots(partner_of(c))
-
     def helper_of(c):
         return [d for d in range(WORLD) if same_chip(c, d) and topo.die(d) != topo.die(c)
-                and all(topo.may_write(d, e) for e in rack_members(c))][0]
+                and all(topo.may_write(d, e) for e in peers_of(c))][0]
 
-    def fan(src, dests, outs, arrive, left):
-        m = topo.mask(core, dests[0])
+    def common(src, dests):
+        m = topo.mask(src, dests[0])
         for d in dests[1:]:
-            m &= topo.mask(core, d)
+            m &= topo.mask(src, d)
+        return m
+
+    def bits(m):
+        return bin(m).count("1")
+
+    def fan(src, dests, out, arrive, left, m):
         ids = [topo.addr(d, core) for d in dests]
         g.remote_dma_fused([RemoteDMATransfer(dst_ids=[DstId(rid=rid, pnc=pid) for rid, pid in ids], dma_engine_mask=m,
-                                              remote_sem=arrive, srcs=[src], dsts=outs)], local_sem=left)
-        return bin(m).count("1")
+                                              remote_sem=arrive, srcs=[src], dsts=[out] * len(dests))], local_sem=left)
+        return bits(m)
+
+    def count(r):
+        return T.cnt[:, 4 * r:4 * r + 1]
 
     rank = T.rank_of(core)
     if rank is None:
@@ -108,193 +83,235 @@ def rank_program(g, core, T, topo):
             if same_chip(core, d) and core == helper_of(d):
                 far = partner_of(d)
                 r = cores.index(far)
-                g.wait_ge(sem.cpeer, bin(topo.mask(far, core)).count("1"))
-                members = rack_slots(d)[1:] + [d]
-                g.wait_ge(sem.lc, fan(T.cnt[:, r:r + 1], members, [T.cnt[:, r:r + 1]] * 4, sem.cpart, sem.lc))
+                peers = peers_of(d)
+                m_off = common(core, peers)
+                m_on = topo.mask(core, d) & ~m_off
+
+                def relay(src, arrive, left):
+                    return fan(src, peers, src, arrive, left, m_off) + fan(src, [d], src, arrive, left, m_on)
+
+                g.wait_ge(sem.cpeer, bits(topo.mask(far, core)))
+                nc = relay(count(r), sem.cpart, sem.lc)
+                g.wait_ge(sem.down, bits(topo.mask(far, core)))
+                nd = relay(T.land[:, r * W:r * W + HW], sem.drel, sem.ld)
+                g.wait_ge(sem.lc, nc)
+                g.wait_ge(sem.ld, nd)
         return
 
     partner = partner_of(core)
-    order = slots_of(core)
-    peers = order[1:4]
-    slot = [order.index(c) for c in cores]
+    prank = cores.index(partner)
+    peers = peers_of(core)
+    own_helper = helper_of(core)
+    far_helper = helper_of(partner)
+    m_peers = common(core, peers)
 
-    def land(k, lo=0, hi=W):
-        return T.land[:, k * W + lo:k * W + hi]
+    def land(r, lo=0, hi=W):
+        return T.land[:, r * W + lo:r * W + hi]
 
-    def across(out, src, arrive, left):
-        rid, pid = topo.addr(partner, core)
-        m = topo.mask(core, partner)
-        g.remote_dma(out, src, arrive, left, pid, rid, m)
-        return bin(m).count("1")
+    def across(dst, piece, arrive, left):
+        rid, pid = topo.addr(dst, core)
+        m = topo.mask(core, dst)
+        g.remote_dma(piece, piece, arrive, left, pid, rid, m)
+        return bits(m)
 
     g.sync.dma_start(T.kin[:], T.keep[:]).then_inc(sem.ldk, 16)
     g.sync.dma_start(T.xin[:, 0:TX], T.x[:]).then_inc(sem.ldx, 16)
 
-    v.memset(T.ones[:], 1.0).then_inc(sem.c1, 1)
-    v.memset(T.run[:, 0:1], 0.0).then_inc(sem.cst, 1)
-    v.memset(T.zsel[:], 0.0).then_inc(sem.cst, 1)
-    v.memset(T.ptab[:, 128:144], 1024.0).then_inc(sem.cst, 1)
-    v.memset(T.xin[:, TX:TX + 16], 0.0).then_inc(sem.cst, 1)
-    v.memset(T.land[:, 8 * W:8 * W + 16], 0.0).then_inc(sem.cst, 1)
-    NCST = 5
-    v.wait_ge(sem.c1, 1)
+    v.memset(T.ones[:], 1.0).then_inc(sem.k0, 1)
+    v.memset(T.dz[:], 0.0).then_inc(sem.k1, 1)
+    v.memset(T.dm[:], 1.0).then_inc(sem.k1, 1)
+    v.memset(T.inv[:], 1.0 / 128.0).then_inc(sem.k5, 1)
+    v.wait_ge(sem.k1, 2)
+    v.memset(T.dz[:, 0:128:16], 1.0).then_inc(sem.k2, 1)
+    v.memset(T.dm[:, 0:128:16], 0.0).then_inc(sem.k2, 1)
+    v.wait_ge(sem.k0, 1)
+    v.wait_ge(sem.k2, 2)
+    v.tensor_tensor_scan(T.hq[:], T.ones[:, 0:128], T.dz[:], -1.0, A.mult, A.add).then_inc(sem.k3, 1)
+    v.tensor_tensor_scan(T.m16[:], T.dm[:], T.dm[:], 0.0, A.mult, A.add).then_inc(sem.k4, 1)
     v.tensor_tensor_scan(T.j2[:], T.ones[:], T.ones[:], -1.0, A.mult, A.add).then_inc(sem.vj2, 1)
-    v.wait_ge(sem.cst, NCST)
-
-    g.wait_ge(sem.c1, 1)
-    g.affine_select(T.half[:], T.ones[:, 0:128], [[-16, 8], [0, 16]], A.is_ge, 0.0, 0, 1).then_inc(sem.gh, 1)
-    g.wait_ge(sem.gh, 1)
-    g.affine_select(T.blk[:], T.half[:], [[16, 8], [0, 16]], A.is_ge, 0.0, 15, -1).then_inc(sem.gblk, 1)
+    t.wait_ge(sem.k5, 1)
+    t.wait_ge(sem.k3, 1)
+    t.matmul(T.b0[:, 1:2], T.hq[:], T.inv[:, 0:1], True, True).then_inc(sem.kp, 1)
+    t.wait_ge(sem.k4, 1)
+    t.matmul(T.b0[:, 2:3], T.m16[:], T.inv[:, 0:1], True, True).then_inc(sem.kp, 1)
+    t.wait_ge(sem.vj2, 1)
+    t.matmul(T.b0[:, 0:1], T.j2[:, 0:128], T.inv[:, 0:1], True, True).then_inc(sem.kp, 1)
+    s.wait_ge(sem.k5, 1)
+    s.activation(T.run[:, 0:1], T.inv[:, 0:1], COPY, scale=0.0).then_inc(sem.cst, 1)
+    s.activation(T.ptab[:, 128:144], T.inv[:, 0:16], COPY, scale=131072.0).then_inc(sem.cst, 1)
+    s.activation(T.xin[:, TX:TX + 16], T.inv[:, 0:16], COPY, scale=0.0).then_inc(sem.cst, 1)
+    NCST = 3
+    g.wait_ge(sem.k0, 1)
+    g.affine_select(T.upto[:], T.ones[:, 0:8], [[-16, 8]], A.is_ge, 0.0, 0, 1).then_inc(sem.gup, 1)
+    g.wait_ge(sem.gup, 1)
+    g.affine_select(T.ind[:], T.upto[:], [[16, 8]], A.is_ge, 0.0, 15, -1).then_inc(sem.gind, 1)
     g.iota(T.j3[:], [[16, 16], [1, 16]], 0, 0, allow_small_or_imprecise_dtypes=True).then_inc(sem.gj, 1)
     g.wait_ge(sem.gblk, 1)
     g.affine_select(T.tri[:], T.blk[:], [[1, 128]], A.is_ge, 0.0, 0, -1).then_inc(sem.gtri, 1)
-    g.affine_select(T.eye[:], T.ones[:, 0:128], [[1, 128]], A.is_equal, 0.0, 0, -1).then_inc(sem.geye, 1)
-
-    v.wait_ge(sem.gblk, 1)
-    v.tensor_copy(T.zsel[:, 15:143:16], T.blk[:, 0:128:16]).then_inc(sem.zs, 1)
 
     v.wait_ge(sem.ldk, 16)
     v.tensor_copy(T.kb[:], T.kin[:]).then_inc(sem.v1, 1)
     v.wait_ge(sem.v1, 1)
     v.tensor_tensor_scan(T.run[:, 1:129], T.ones[:, 0:128], T.kb[:], 0.0, A.mult, A.add).then_inc(sem.v2, 1)
+    v.wait_ge(sem.kp, 3)
+    v.wait_ge(sem.k3, 1)
+    v.wait_ge(sem.k4, 1)
+    v.wait_ge(sem.vj2, 1)
+    v.tensor_scalar(T.blk[:], T.hq[:], T.b0[:, 1:2], None, A.is_equal).then_inc(sem.gblk, 1)
+    v.tensor_scalar(T.eye[:], T.j2[:, 0:128], T.b0[:, 0:1], None, A.is_equal).then_inc(sem.geye, 1)
+    v.tensor_scalar(T.mb[:], T.m16[:], T.b0[:, 2:3], None, A.is_equal).then_inc(sem.gmb, 1)
 
-    t.wait_ge(sem.gblk, 1)
-    t.wait_ge(sem.cst, NCST)
-    t.wait_ge(sem.v1, 1)
+    t.wait_ge(sem.gind, 1)
     t.wait_ge(sem.v2, 1)
-    t.matmul(T.pcs[:, 0:8], T.run[:, 1:129], T.blk[:, 0:128:16], True, True).then_inc(sem.p1, 1)
-    t.matmul(T.pcn[:, 0:1], T.blk[:], T.run[:, 128:129], True, True).then_inc(sem.p2, 1)
-    t.matmul(T.pps[:, 0:128], T.blk[:], T.run[:, 0:128], True, False)
+    t.matmul(T.b1[:, 0:8], T.run[:, 1:129], T.ind[:], True, True).then_inc(sem.p1, 1)
+    t.wait_ge(sem.gblk, 1)
+    t.matmul(T.b2[:, 0:1], T.blk[:], T.run[:, 128:129], True, True).then_inc(sem.p2, 1)
+    t.wait_ge(sem.cst, NCST)
+    t.matmul(T.b3[:, 0:128], T.blk[:], T.run[:, 0:128], True, False)
     t.wait_ge(sem.gtri, 1)
-    t.matmul(T.pps[:, 0:128], T.tri[:], T.kb[:], False, True).then_inc(sem.p3, 1)
+    t.wait_ge(sem.v1, 1)
+    t.matmul(T.b3[:, 0:128], T.tri[:], T.kb[:], False, True).then_inc(sem.p3, 1)
 
     s.wait_ge(sem.p2, 1)
-    s.activation(T.cown[:, 0:1], T.pcn[:, 0:1], COPY).then_inc(sem.s1, 1)
-    s.wait_ge(sem.cst, NCST)
+    s.activation(count(rank), T.b2[:, 0:1], COPY).then_inc(sem.s1, 1)
     s.wait_ge(sem.p3, 1)
-    s.activation(T.ptab[:, 0:128], T.pps[:, 0:128], COPY).then_inc(sem.s2, 1)
+    s.activation(T.ptab[:, 0:128], T.b3[:, 0:128], COPY).then_inc(sem.s2, 1)
 
     v.wait_ge(sem.p1, 1)
-    v.tensor_copy(T.colc[:], T.pcs[:, 0:8]).then_inc(sem.v3, 1)
+    v.tensor_copy(T.colc[:], T.b1[:, 0:8]).then_inc(sem.v3, 1)
     v.wait_ge(sem.gj, 1)
     v.wait_ge(sem.v3, 1)
     for lo, done in ((0, sem.v4), (8, sem.v5)):
         for h in range(8):
             v.tensor_scalar(T.cge[:, lo:lo + 8, 16 * h:16 * h + 16], T.j3[:, lo:lo + 8, :], T.colc[:, h:h + 1], None,
                             A.is_ge).then_inc(done, 1)
-    for lo, ready, out, done in ((0, sem.v4, T.pca, sem.p4), (8, sem.v5, T.pcb, sem.p5)):
+    for lo, ready, out, done in ((0, sem.v4, T.b4, sem.p4), (8, sem.v5, T.b5, sem.p5)):
         t.wait_ge(ready, 8)
         for b in range(8):
             t.matmul(out[:, b:b + 1], T.cge[:, lo + b, :], T.ones[:, 0:1], True, True).then_inc(done, 1)
 
+    v.wait_ge(sem.cst, NCST)
     v.wait_ge(sem.p4, 8)
-    v.tensor_copy(T.offa[:], T.pca[:, 0:8]).then_inc(sem.v6, 1)
+    v.tensor_copy(T.offa[:], T.b4[:, 0:8]).then_inc(sem.v6, 1)
     v.wait_ge(sem.v6, 1)
-    v.wait_ge(sem.vj2, 1)
     v.wait_ge(sem.s2, 1)
-    v.tensor_tensor(T.ile[:, 0:128], T.ptab[:, 0:129].indirect(T.offa[:, 0:8]), T.j2[:, 0:128], A.is_le).then_inc(sem.v7, 1)
+    v.tensor_tensor(T.ile[:, 0:128], T.ptab[:, 0:129].indirect(T.offa[:, 0:8]), T.j2[:, 0:128], A.is_le).then_inc(sem.v7a, 1)
     v.wait_ge(sem.p5, 8)
-    v.tensor_copy(T.offb[:], T.pcb[:, 0:8]).then_inc(sem.v6b, 1)
+    v.tensor_copy(T.offb[:], T.b5[:, 0:8]).then_inc(sem.v6b, 1)
     v.wait_ge(sem.v6b, 1)
     v.tensor_tensor(T.ile[:, 128:256], T.ptab[:, 0:129].indirect(T.offb[:, 0:8]), T.j2[:, 128:256],
-                    A.is_le).then_inc(sem.v7, 1)
+                    A.is_le).then_inc(sem.v7b, 1)
 
     s.wait_ge(sem.v6, 1)
-    s.activation(T.cbf[:, 0:8], T.pca[:, 0:8], COPY, scale=16.0).then_inc(sem.s3, 1)
+    s.activation(T.cbf[:, 0:8], T.b4[:, 0:8], COPY, scale=16.0).then_inc(sem.s3a, 1)
     s.wait_ge(sem.v6b, 1)
-    s.activation(T.cbf[:, 8:16], T.pcb[:, 0:8], COPY, scale=16.0).then_inc(sem.s3, 1)
+    s.activation(T.cbf[:, 8:16], T.b5[:, 0:8], COPY, scale=16.0).then_inc(sem.s3b, 1)
 
     t.wait_ge(sem.geye, 1)
-    t.wait_ge(sem.zs, 1)
-    t.wait_ge(sem.s3, 2)
-    t.matmul(T.pis[:, 0:16], T.eye[:], T.cbf[:], True, False)
-    t.wait_ge(sem.v7, 2)
-    for a in range(16):
-        mm = t.matmul(T.pis[:, 0:16], T.zsel[:, 15 - a:143 - a], T.ile[:, a:256:16], False, a == 15)
-        if a == 15:
-            mm.then_inc(sem.p6, 1)
+    t.wait_ge(sem.gmb, 1)
+    pA, pB = T.b0[:, 0:8], T.b1[:, 0:8]
+    t.wait_ge(sem.s3a, 1)
+    t.matmul(pA, T.eye[:], T.cbf[:, 0:8], True, False)
+    t.wait_ge(sem.v7a, 1)
+    t.matmul(T.b6[:, 0:128], T.ile[:, 0:128], T.blk[:], True, True).then_inc(sem.pya, 1)
+    t.wait_ge(sem.s3b, 1)
+    t.matmul(pB, T.eye[:], T.cbf[:, 8:16], True, False)
+    t.wait_ge(sem.v7b, 1)
+    t.matmul(T.b7[:, 0:128], T.ile[:, 128:256], T.blk[:], True, True).then_inc(sem.pyb, 1)
+    t.wait_ge(sem.v8a, 1)
+    t.matmul(pA, T.ym[:, 0:128], T.ind[:], False, True).then_inc(sem.p6a, 1)
+    t.wait_ge(sem.v8b, 1)
+    t.matmul(pB, T.ym[:, 128:256], T.ind[:], False, True).then_inc(sem.p6b, 1)
 
-    v.wait_ge(sem.p6, 1)
-    v.tensor_copy(T.lst[:], T.pis[:, 0:16]).then_inc(sem.v9, 1)
+    v.wait_ge(sem.gmb, 1)
+    v.wait_ge(sem.pya, 1)
+    v.tensor_tensor(T.ym[:, 0:128], T.b6[:, 0:128], T.mb[:], A.mult).then_inc(sem.v8a, 1)
+    v.wait_ge(sem.pyb, 1)
+    v.tensor_tensor(T.ym[:, 128:256], T.b7[:, 0:128], T.mb[:], A.mult).then_inc(sem.v8b, 1)
     Q = W // 4
+    v.wait_ge(sem.p6a, 1)
+    v.tensor_copy(T.lst[:, 0:8], pA).then_inc(sem.v9a, 1)
     for q in (v, s):
-        q.wait_ge(sem.v9, 1)
+        q.wait_ge(sem.cst, NCST)
         q.wait_ge(sem.ldx, 16)
-    for lo, done in ((0, sem.pk), (HW, sem.pk2)):
-        v.tensor_copy(land(0, lo, lo + Q), T.xin[:].indirect(T.lst[:, lo // 16:(lo + Q) // 16])).then_inc(done, 1)
-        s.activation(land(0, lo + Q, lo + HW), T.xin[:].indirect(T.lst[:, (lo + Q) // 16:(lo + HW) // 16]),
-                     COPY).then_inc(done, 1)
+        q.wait_ge(sem.v9a, 1)
+    v.tensor_copy(land(rank, 0, Q), T.xin[:].indirect(T.lst[:, 0:4])).then_inc(sem.pk, 1)
+    s.activation(land(rank, Q, HW), T.xin[:].indirect(T.lst[:, 4:8]), COPY).then_inc(sem.pk, 1)
+    v.wait_ge(sem.p6b, 1)
+    v.tensor_copy(T.lst[:, 8:16], pB).then_inc(sem.v9b, 1)
+    v.wait_ge(sem.v9b, 1)
+    s.wait_ge(sem.v9b, 1)
+    v.tensor_copy(land(rank, HW, HW + Q), T.xin[:].indirect(T.lst[:, 8:12])).then_inc(sem.pk2, 1)
+    s.activation(land(rank, HW + Q, W), T.xin[:].indirect(T.lst[:, 12:16]), COPY).then_inc(sem.pk2, 1)
 
+    n_off = bits(common(own_helper, peers))
+    n_on = bits(topo.mask(own_helper, core) & ~common(own_helper, peers))
     g.wait_ge(sem.s1, 1)
-    ne = fan(T.cown[:, 0:1], peers + [helper_of(partner)], [T.cnt[:, rank:rank + 1]] * 4, sem.cpeer, sem.lc)
-    g.iota(T.pcol[:], [[0, 8]], 0, 1).then_inc(sem.gjw, 1)
-    g.iota(T.jb[:], [[16, 128]], 0, 0, allow_small_or_imprecise_dtypes=True).then_inc(sem.gjw, 1)
+    nlc = across(far_helper, count(rank), sem.cpeer, sem.lc)
+    ne = fan(count(rank), peers, count(rank), sem.cpeer, sem.lc, m_peers)
     g.wait_ge(sem.pk, 2)
-    nx = across(land(4, 0, HW), land(0, 0, HW), sem.down, sem.ld)
+    nld = across(far_helper, land(rank, 0, HW), sem.down, sem.ld)
     g.wait_ge(sem.pk2, 2)
-    nld = nx + across(land(4, HW, W), land(0, HW, W), sem.down2, sem.ld)
-    nld += fan(land(0), peers, [land(slots_of(d).index(core)) for d in peers], sem.dpeer, sem.ld)
-    for lo, arrived in ((0, sem.down), (HW, sem.down2)):
-        g.wait_ge(arrived, nx)
-        nld += fan(land(4, lo, lo + HW), peers, [land(slots_of(d).index(partner), lo, lo + HW) for d in peers],
-                   sem.drel, sem.ld)
-    g.wait_ge(sem.lc, ne)
+    nx = across(partner, land(rank, HW, W), sem.down2, sem.ld)
+    nld += nx + fan(land(rank), peers, land(rank), sem.dpeer, sem.ld, m_peers)
+    g.wait_ge(sem.down2, nx)
+    nld += fan(land(prank, HW, W), peers, land(prank, HW, W), sem.drel, sem.ld, m_peers)
+    g.wait_ge(sem.lc, nlc + ne)
     g.wait_ge(sem.ld, nld)
 
-    v.wait_ge(sem.gjw, 2)
-    v.tensor_scalar(T.pmod[:], T.pcol[:], 15, None, A.bitwise_and).then_inc(sem.vp1, 1)
-    v.wait_ge(sem.vp1, 1)
-    v.tensor_copy(T.pmf[:], T.pmod[:]).then_inc(sem.vp2, 1)
-    v.wait_ge(sem.vp2, 1)
-    v.tensor_scalar(T.jw[:], T.jb[:], T.pmf[:, 0:1], float(W * slot[0]), A.add, A.add).then_inc(sem.vp3, 1)
-    v.tensor_scalar(T.offf[:], T.jb[:], T.pmf[:, 0:1], None, A.add).then_inc(sem.vp3, 1)
+    v.memset(T.land[:, 8 * W:8 * W + 16], 0.0).then_inc(sem.f1, 1)
     v.memset(T.one8[:], 1.0).then_inc(sem.f1, 1)
-    for r in range(8):
-        d = float(W * (slot[r + 1] - slot[r])) if r < 7 else 8192.0
-        v.memset(T.step[:, r:r + 1], d).then_inc(sem.f1, 1)
-    v.wait_ge(sem.f1, 9)
+    v.memset(T.dlt[:, 7:8], 8192.0).then_inc(sem.f1, 1)
+    v.tensor_scalar(T.r16[:], T.j2[:, 0:128], 16.0, None, A.mult).then_inc(sem.kr, 1)
+    t.wait_ge(sem.kr, 1)
+    t.wait_ge(sem.s1, 1)
+    for out, stop in ((T.b2, True), (T.b3, False)):
+        t.matmul(out[:, 0:128], T.m16[:], T.inv[:], True, False)
+        mm = t.matmul(out[:, 0:128], T.inv[:], T.r16[:], False, stop)
+        if stop:
+            mm.then_inc(sem.pj, 1)
+    v.wait_ge(sem.pj, 1)
+    v.tensor_copy(T.ju[:], T.b2[:, 0:128]).then_inc(sem.f2, 1)
+    v.wait_ge(sem.f1, 3)
     v.wait_ge(sem.s1, 1)
     v.wait_ge(sem.cpeer, 3 * ne)
-    v.wait_ge(sem.cpart, 4 * ne)
-    v.tensor_copy(T.cnt[:, rank:rank + 1], T.cown[:, 0:1]).then_inc(sem.f2, 1)
-    v.wait_ge(sem.f2, 1)
-    v.tensor_tensor_scan(T.ends[:], T.one8[:], T.cnt[:], 0.0, A.mult, A.add).then_inc(sem.f3, 1)
-    v.tensor_tensor(T.dlt[:], T.step[:], T.cnt[:], A.subtract).then_inc(sem.f3, 1)
+    v.wait_ge(sem.cpart, 3 * n_off + n_on)
+    v.tensor_tensor_scan(T.ends[:], T.one8[:], T.cnt[:, 0:32:4], 0.0, A.mult, A.add).then_inc(sem.f3, 1)
+    v.tensor_scalar(T.dlt[:, 0:7], T.cnt[:, 0:28:4], -1.0, float(W), A.mult, A.add).then_inc(sem.f3, 1)
     v.wait_ge(sem.f3, 2)
-    v.wait_ge(sem.vp3, 2)
+    v.wait_ge(sem.f2, 1)
     for r in range(8):
-        v.tensor_scalar(T.term[:, 128 * r:128 * r + 128], T.offf[:], T.ends[:, r:r + 1], T.dlt[:, r:r + 1],
+        v.tensor_scalar(T.term[:, 128 * r:128 * r + 128], T.ju[:], T.ends[:, r:r + 1], T.dlt[:, r:r + 1],
                         A.is_ge, A.mult).then_inc(sem.f4, 1)
-    v.wait_ge(sem.f4, 8)
-    v.tensor_tensor(T.sum4[:], T.term[:, 0:512], T.term[:, 512:1024], A.add).then_inc(sem.f5, 1)
-    v.wait_ge(sem.f5, 1)
-    v.tensor_tensor(T.sum2[:], T.sum4[:, 0:256], T.sum4[:, 256:512], A.add).then_inc(sem.f6, 1)
-    v.wait_ge(sem.f6, 1)
-    v.tensor_tensor(T.sum1[:], T.sum2[:, 0:128], T.sum2[:, 128:256], A.add).then_inc(sem.f7, 1)
-    v.wait_ge(sem.f7, 1)
-    v.tensor_tensor(T.term[:, 0:128], T.sum1[:], T.jw[:], A.add).then_inc(sem.f8, 1)
-    v.wait_ge(sem.f8, 1)
-    v.tensor_scalar(T.fin[:], T.term[:, 0:128], float(ZC), None, A.min).then_inc(sem.f9, 1)
+        t.wait_ge(sem.f4, r + 1)
+        mm = t.matmul(T.b3[:, 0:128], T.eye[:], T.term[:, 128 * r:128 * r + 128], False, r == 7)
+    mm.then_inc(sem.pf, 1)
+    v.wait_ge(sem.pf, 1)
+    v.tensor_scalar(T.fin[:], T.b3[:, 0:128], float(ZC), None, A.min).then_inc(sem.f9, 1)
 
     for q in (v, s):
         q.wait_ge(sem.f9, 1)
         q.wait_ge(sem.pk, 2)
         q.wait_ge(sem.pk2, 2)
         q.wait_ge(sem.dpeer, 3 * ne)
-        q.wait_ge(sem.down, nx)
         q.wait_ge(sem.down2, nx)
-        q.wait_ge(sem.drel, 6 * ne)
-    H = TX // 4
+        q.wait_ge(sem.drel, 3 * ne + 3 * n_off + n_on)
     win = T.land[:]
-    for n in (0, 1):
-        v.tensor_copy(T.yb[:, n * H:(n + 1) * H],
-                      win.indirect(T.fin[:, n * H // 16:(n + 1) * H // 16])).then_inc((sem.y1, sem.y2)[n], 1)
-        m = n + 2
-        s.activation(T.yb[:, m * H:(m + 1) * H], win.indirect(T.fin[:, m * H // 16:(m + 1) * H // 16]),
-                     COPY).then_inc((sem.y3, sem.y4)[n], 1)
-    for m, done in ((0, sem.y1), (2, sem.y3), (1, sem.y2)):
-        g.sync.wait_ge(done, 1)
-        g.sync.dma_start(T.y[:, m * H:(m + 1) * H], T.yb[:, m * H:(m + 1) * H]).then_inc(sem.st, 16)
-    s.wait_ge(sem.y4, 1)
-    s.dma_start(T.y[:, 3 * H:4 * H], T.yb[:, 3 * H:4 * H]).then_inc(sem.st, 16)
-    g.sync.wait_ge(sem.st, 64)
+    stores = []
+    lo = 0
+    for n, w in enumerate(PIECES):
+        for q, base in ((v, 0), (s, TX // 2)):
+            a, b = base + lo, base + lo + w
+            src = win.indirect(T.fin[:, a // 16:b // 16])
+            done = sem["y%s%d" % ("v" if q is v else "s", n)]
+            if q is v:
+                v.tensor_copy(T.yb[:, a:b], src).then_inc(done, 1)
+            else:
+                s.activation(T.yb[:, a:b], src, COPY).then_inc(done, 1)
+            stores.append((a, b, done))
+        lo += w
+    for k, (a, b, done) in enumerate(stores):
+        q = s if k == len(stores) - 1 else g.sync
+        q.wait_ge(done, 1)
+        q.dma_start(T.y[:, a:b], T.yb[:, a:b]).then_inc(sem.st, 16)
+    g.sync.wait_ge(sem.st, 16 * len(stores))

from concourse.bass import DstId, RemoteDMATransfer
from concourse.mybir import AluOpType, ActivationFunctionType

W = 256
HW = W // 2
TX = 2048
ZC = 2048
WORLD = 512
PIECES = (288, 448, 288)


def _sb(cols, kind="bfloat16"):
    return ("sbuf", [128] + cols, kind)


SCRATCH = {
    "kin": _sb([128], "int32"), "xin": _sb([TX + 16]), "kb": _sb([128]), "run": _sb([144]),
    "ones": _sb([256]), "inv": _sb([128]), "dz": _sb([128]), "dm": _sb([128]), "hq": _sb([128]), "m16": _sb([128]),
    "r16": _sb([128]), "upto": _sb([8]), "ind": _sb([8]), "blk": _sb([128]), "tri": _sb([128]), "eye": _sb([128]),
    "mb": _sb([128]), "j3": _sb([16, 16]), "j2": _sb([256]), "colc": _sb([8]), "cge": _sb([16, 128]),
    "ptab": _sb([144]), "offa": _sb([8], "uint16"), "offb": _sb([8], "uint16"), "cbf": _sb([16]), "ile": _sb([256]),
    "ym": _sb([256]), "lst": _sb([16], "uint16"), "land": _sb([8 * W + 16]), "cnt": _sb([32], "float32"),
    "ju": _sb([128], "uint16"), "ends": _sb([8], "float32"), "dlt": _sb([8], "float32"), "one8": _sb([8], "float32"),
    "term": _sb([1024]), "fin": _sb([128], "uint16"), "yb": _sb([TX]),
}
for _k in range(8):
    SCRATCH["b%d" % _k] = ("psum", [128, 512], "float32")
SEMAPHORES = ["ldk", "ldx", "cst", "k0", "k1", "k2", "k3", "k4", "k5", "kp", "kr", "gup", "gind", "gj", "gblk", "gtri",
              "geye", "gmb",
              "v1", "v2", "v3", "v4", "v5", "v6", "v6b", "v7a", "v7b", "v8a", "v8b", "v9a", "v9b", "vj2",
              "p1", "p2", "p3", "p4", "p5", "p6a", "p6b", "pya", "pyb", "pj", "pf", "s1", "s2", "s3a", "s3b", "pk", "pk2",
              "cpeer", "cpart", "dpeer", "down", "down2", "drel", "lc", "ld",
              "f1", "f2", "f3", "f4", "f9",
              "yv0", "yv1", "yv2", "ys0", "ys1", "ys2", "st"]


def rank_program(g, core, T, topo):
    A = AluOpType
    COPY = ActivationFunctionType.Copy
    sem = T.sem
    v, s, t = g.vector, g.scalar, g.tensor

    cores = list(T.cores)

    def same_chip(a, b):
        return topo.host(a) == topo.host(b) and topo.chip(a) == topo.chip(b)

    def rack_of(c):
        return topo.rack(topo.host(c))

    def peers_of(c):
        m = [d for d in cores if rack_of(d) == rack_of(c)]
        return [m[m.index(c) ^ k] for k in range(1, 4)]

    def partner_of(c):
        return [d for d in cores if rack_of(d) != rack_of(c) and topo.chip(d) == topo.chip(c) and topo.may_write(c, d)][0]

    def helper_of(c):
        return [d for d in range(WORLD) if same_chip(c, d) and topo.die(d) != topo.die(c)
                and all(topo.may_write(d, e) for e in peers_of(c))][0]

    def common(src, dests):
        m = topo.mask(src, dests[0])
        for d in dests[1:]:
            m &= topo.mask(src, d)
        return m

    def bits(m):
        return bin(m).count("1")

    def fan(src, dests, out, arrive, left, m):
        ids = [topo.addr(d, core) for d in dests]
        g.remote_dma_fused([RemoteDMATransfer(dst_ids=[DstId(rid=rid, pnc=pid) for rid, pid in ids], dma_engine_mask=m,
                                              remote_sem=arrive, srcs=[src], dsts=[out] * len(dests))], local_sem=left)
        return bits(m)

    def count(r):
        return T.cnt[:, 4 * r:4 * r + 1]

    rank = T.rank_of(core)
    if rank is None:
        for d in cores:
            if same_chip(core, d) and core == helper_of(d):
                far = partner_of(d)
                r = cores.index(far)
                peers = peers_of(d)
                m_off = common(core, peers)
                m_on = topo.mask(core, d) & ~m_off

                def relay(src, arrive, left):
                    return fan(src, peers, src, arrive, left, m_off) + fan(src, [d], src, arrive, left, m_on)

                g.wait_ge(sem.cpeer, bits(topo.mask(far, core)))
                nc = relay(count(r), sem.cpart, sem.lc)
                g.wait_ge(sem.down, bits(topo.mask(far, core)))
                nd = relay(T.land[:, r * W:r * W + HW], sem.drel, sem.ld)
                g.wait_ge(sem.lc, nc)
                g.wait_ge(sem.ld, nd)
        return

    partner = partner_of(core)
    prank = cores.index(partner)
    peers = peers_of(core)
    own_helper = helper_of(core)
    far_helper = helper_of(partner)
    m_peers = common(core, peers)

    def land(r, lo=0, hi=W):
        return T.land[:, r * W + lo:r * W + hi]

    def across(dst, piece, arrive, left):
        rid, pid = topo.addr(dst, core)
        m = topo.mask(core, dst)
        g.remote_dma(piece, piece, arrive, left, pid, rid, m)
        return bits(m)

    g.sync.dma_start(T.kin[:], T.keep[:]).then_inc(sem.ldk, 16)
    g.sync.dma_start(T.xin[:, 0:TX], T.x[:]).then_inc(sem.ldx, 16)

    v.memset(T.ones[:], 1.0).then_inc(sem.k0, 1)
    v.memset(T.dz[:], 0.0).then_inc(sem.k1, 1)
    v.memset(T.dm[:], 1.0).then_inc(sem.k1, 1)
    v.memset(T.inv[:], 1.0 / 128.0).then_inc(sem.k5, 1)
    v.wait_ge(sem.k1, 2)
    v.memset(T.dz[:, 0:128:16], 1.0).then_inc(sem.k2, 1)
    v.memset(T.dm[:, 0:128:16], 0.0).then_inc(sem.k2, 1)
    v.wait_ge(sem.k0, 1)
    v.wait_ge(sem.k2, 2)
    v.tensor_tensor_scan(T.hq[:], T.ones[:, 0:128], T.dz[:], -1.0, A.mult, A.add).then_inc(sem.k3, 1)
    v.tensor_tensor_scan(T.m16[:], T.dm[:], T.dm[:], 0.0, A.mult, A.add).then_inc(sem.k4, 1)
    v.tensor_tensor_scan(T.j2[:], T.ones[:], T.ones[:], -1.0, A.mult, A.add).then_inc(sem.vj2, 1)
    t.wait_ge(sem.k5, 1)
    t.wait_ge(sem.k3, 1)
    t.matmul(T.b0[:, 1:2], T.hq[:], T.inv[:, 0:1], True, True).then_inc(sem.kp, 1)
    t.wait_ge(sem.k4, 1)
    t.matmul(T.b0[:, 2:3], T.m16[:], T.inv[:, 0:1], True, True).then_inc(sem.kp, 1)
    t.wait_ge(sem.vj2, 1)
    t.matmul(T.b0[:, 0:1], T.j2[:, 0:128], T.inv[:, 0:1], True, True).then_inc(sem.kp, 1)
    s.wait_ge(sem.k5, 1)
    s.activation(T.run[:, 0:1], T.inv[:, 0:1], COPY, scale=0.0).then_inc(sem.cst, 1)
    s.activation(T.ptab[:, 128:144], T.inv[:, 0:16], COPY, scale=131072.0).then_inc(sem.cst, 1)
    s.activation(T.xin[:, TX:TX + 16], T.inv[:, 0:16], COPY, scale=0.0).then_inc(sem.cst, 1)
    NCST = 3
    g.wait_ge(sem.k0, 1)
    g.affine_select(T.upto[:], T.ones[:, 0:8], [[-16, 8]], A.is_ge, 0.0, 0, 1).then_inc(sem.gup, 1)
    g.wait_ge(sem.gup, 1)
    g.affine_select(T.ind[:], T.upto[:], [[16, 8]], A.is_ge, 0.0, 15, -1).then_inc(sem.gind, 1)
    g.iota(T.j3[:], [[16, 16], [1, 16]], 0, 0, allow_small_or_imprecise_dtypes=True).then_inc(sem.gj, 1)
    g.wait_ge(sem.gblk, 1)
    g.affine_select(T.tri[:], T.blk[:], [[1, 128]], A.is_ge, 0.0, 0, -1).then_inc(sem.gtri, 1)

    v.wait_ge(sem.ldk, 16)
    v.tensor_copy(T.kb[:], T.kin[:]).then_inc(sem.v1, 1)
    v.wait_ge(sem.v1, 1)
    v.tensor_tensor_scan(T.run[:, 1:129], T.ones[:, 0:128], T.kb[:], 0.0, A.mult, A.add).then_inc(sem.v2, 1)
    v.wait_ge(sem.kp, 3)
    v.wait_ge(sem.k3, 1)
    v.wait_ge(sem.k4, 1)
    v.wait_ge(sem.vj2, 1)
    v.tensor_scalar(T.blk[:], T.hq[:], T.b0[:, 1:2], None, A.is_equal).then_inc(sem.gblk, 1)
    v.tensor_scalar(T.eye[:], T.j2[:, 0:128], T.b0[:, 0:1], None, A.is_equal).then_inc(sem.geye, 1)
    v.tensor_scalar(T.mb[:], T.m16[:], T.b0[:, 2:3], None, A.is_equal).then_inc(sem.gmb, 1)

    t.wait_ge(sem.gind, 1)
    t.wait_ge(sem.v2, 1)
    t.matmul(T.b1[:, 0:8], T.run[:, 1:129], T.ind[:], True, True).then_inc(sem.p1, 1)
    t.wait_ge(sem.gblk, 1)
    t.matmul(T.b2[:, 0:1], T.blk[:], T.run[:, 128:129], True, True).then_inc(sem.p2, 1)
    t.wait_ge(sem.cst, NCST)
    t.matmul(T.b3[:, 0:128], T.blk[:], T.run[:, 0:128], True, False)
    t.wait_ge(sem.gtri, 1)
    t.wait_ge(sem.v1, 1)
    t.matmul(T.b3[:, 0:128], T.tri[:], T.kb[:], False, True).then_inc(sem.p3, 1)

    s.wait_ge(sem.p2, 1)
    s.activation(count(rank), T.b2[:, 0:1], COPY).then_inc(sem.s1, 1)
    s.wait_ge(sem.p3, 1)
    s.activation(T.ptab[:, 0:128], T.b3[:, 0:128], COPY).then_inc(sem.s2, 1)

    v.wait_ge(sem.p1, 1)
    v.tensor_copy(T.colc[:], T.b1[:, 0:8]).then_inc(sem.v3, 1)
    v.wait_ge(sem.gj, 1)
    v.wait_ge(sem.v3, 1)
    for lo, done in ((0, sem.v4), (8, sem.v5)):
        for h in range(8):
            v.tensor_scalar(T.cge[:, lo:lo + 8, 16 * h:16 * h + 16], T.j3[:, lo:lo + 8, :], T.colc[:, h:h + 1], None,
                            A.is_ge).then_inc(done, 1)
    for lo, ready, out, done in ((0, sem.v4, T.b4, sem.p4), (8, sem.v5, T.b5, sem.p5)):
        t.wait_ge(ready, 8)
        for b in range(8):
            t.matmul(out[:, b:b + 1], T.cge[:, lo + b, :], T.ones[:, 0:1], True, True).then_inc(done, 1)

    v.wait_ge(sem.cst, NCST)
    v.wait_ge(sem.p4, 8)
    v.tensor_copy(T.offa[:], T.b4[:, 0:8]).then_inc(sem.v6, 1)
    v.wait_ge(sem.v6, 1)
    v.wait_ge(sem.s2, 1)
    v.tensor_tensor(T.ile[:, 0:128], T.ptab[:, 0:129].indirect(T.offa[:, 0:8]), T.j2[:, 0:128], A.is_le).then_inc(sem.v7a, 1)
    v.wait_ge(sem.p5, 8)
    v.tensor_copy(T.offb[:], T.b5[:, 0:8]).then_inc(sem.v6b, 1)
    v.wait_ge(sem.v6b, 1)
    v.tensor_tensor(T.ile[:, 128:256], T.ptab[:, 0:129].indirect(T.offb[:, 0:8]), T.j2[:, 128:256],
                    A.is_le).then_inc(sem.v7b, 1)

    s.wait_ge(sem.v6, 1)
    s.activation(T.cbf[:, 0:8], T.b4[:, 0:8], COPY, scale=16.0).then_inc(sem.s3a, 1)
    s.wait_ge(sem.v6b, 1)
    s.activation(T.cbf[:, 8:16], T.b5[:, 0:8], COPY, scale=16.0).then_inc(sem.s3b, 1)

    t.wait_ge(sem.geye, 1)
    t.wait_ge(sem.gmb, 1)
    pA, pB = T.b0[:, 0:8], T.b1[:, 0:8]
    t.wait_ge(sem.s3a, 1)
    t.matmul(pA, T.eye[:], T.cbf[:, 0:8], True, False)
    t.wait_ge(sem.v7a, 1)
    t.matmul(T.b6[:, 0:128], T.ile[:, 0:128], T.blk[:], True, True).then_inc(sem.pya, 1)
    t.wait_ge(sem.s3b, 1)
    t.matmul(pB, T.eye[:], T.cbf[:, 8:16], True, False)
    t.wait_ge(sem.v7b, 1)
    t.matmul(T.b7[:, 0:128], T.ile[:, 128:256], T.blk[:], True, True).then_inc(sem.pyb, 1)
    t.wait_ge(sem.v8a, 1)
    t.matmul(pA, T.ym[:, 0:128], T.ind[:], False, True).then_inc(sem.p6a, 1)
    t.wait_ge(sem.v8b, 1)
    t.matmul(pB, T.ym[:, 128:256], T.ind[:], False, True).then_inc(sem.p6b, 1)

    v.wait_ge(sem.gmb, 1)
    v.wait_ge(sem.pya, 1)
    v.tensor_tensor(T.ym[:, 0:128], T.b6[:, 0:128], T.mb[:], A.mult).then_inc(sem.v8a, 1)
    v.wait_ge(sem.pyb, 1)
    v.tensor_tensor(T.ym[:, 128:256], T.b7[:, 0:128], T.mb[:], A.mult).then_inc(sem.v8b, 1)
    Q = W // 4
    v.wait_ge(sem.p6a, 1)
    v.tensor_copy(T.lst[:, 0:8], pA).then_inc(sem.v9a, 1)
    for q in (v, s):
        q.wait_ge(sem.cst, NCST)
        q.wait_ge(sem.ldx, 16)
        q.wait_ge(sem.v9a, 1)
    v.tensor_copy(land(rank, 0, Q), T.xin[:].indirect(T.lst[:, 0:4])).then_inc(sem.pk, 1)
    s.activation(land(rank, Q, HW), T.xin[:].indirect(T.lst[:, 4:8]), COPY).then_inc(sem.pk, 1)
    v.wait_ge(sem.p6b, 1)
    v.tensor_copy(T.lst[:, 8:16], pB).then_inc(sem.v9b, 1)
    v.wait_ge(sem.v9b, 1)
    s.wait_ge(sem.v9b, 1)
    v.tensor_copy(land(rank, HW, HW + Q), T.xin[:].indirect(T.lst[:, 8:12])).then_inc(sem.pk2, 1)
    s.activation(land(rank, HW + Q, W), T.xin[:].indirect(T.lst[:, 12:16]), COPY).then_inc(sem.pk2, 1)

    n_off = bits(common(own_helper, peers))
    n_on = bits(topo.mask(own_helper, core) & ~common(own_helper, peers))
    g.wait_ge(sem.s1, 1)
    nlc = across(far_helper, count(rank), sem.cpeer, sem.lc)
    ne = fan(count(rank), peers, count(rank), sem.cpeer, sem.lc, m_peers)
    g.wait_ge(sem.pk, 2)
    nld = across(far_helper, land(rank, 0, HW), sem.down, sem.ld)
    g.wait_ge(sem.pk2, 2)
    nx = across(partner, land(rank, HW, W), sem.down2, sem.ld)
    nld += nx + fan(land(rank), peers, land(rank), sem.dpeer, sem.ld, m_peers)
    g.wait_ge(sem.down2, nx)
    nld += fan(land(prank, HW, W), peers, land(prank, HW, W), sem.drel, sem.ld, m_peers)
    g.wait_ge(sem.lc, nlc + ne)
    g.wait_ge(sem.ld, nld)

    v.memset(T.land[:, 8 * W:8 * W + 16], 0.0).then_inc(sem.f1, 1)
    v.memset(T.one8[:], 1.0).then_inc(sem.f1, 1)
    v.memset(T.dlt[:, 7:8], 8192.0).then_inc(sem.f1, 1)
    v.tensor_scalar(T.r16[:], T.j2[:, 0:128], 16.0, None, A.mult).then_inc(sem.kr, 1)
    t.wait_ge(sem.kr, 1)
    t.wait_ge(sem.s1, 1)
    for out, stop in ((T.b2, True), (T.b3, False)):
        t.matmul(out[:, 0:128], T.m16[:], T.inv[:], True, False)
        mm = t.matmul(out[:, 0:128], T.inv[:], T.r16[:], False, stop)
        if stop:
            mm.then_inc(sem.pj, 1)
    v.wait_ge(sem.pj, 1)
    v.tensor_copy(T.ju[:], T.b2[:, 0:128]).then_inc(sem.f2, 1)
    v.wait_ge(sem.f1, 3)
    v.wait_ge(sem.s1, 1)
    v.wait_ge(sem.cpeer, 3 * ne)
    v.wait_ge(sem.cpart, 3 * n_off + n_on)
    v.tensor_tensor_scan(T.ends[:], T.one8[:], T.cnt[:, 0:32:4], 0.0, A.mult, A.add).then_inc(sem.f3, 1)
    v.tensor_scalar(T.dlt[:, 0:7], T.cnt[:, 0:28:4], -1.0, float(W), A.mult, A.add).then_inc(sem.f3, 1)
    v.wait_ge(sem.f3, 2)
    v.wait_ge(sem.f2, 1)
    for r in range(8):
        v.tensor_scalar(T.term[:, 128 * r:128 * r + 128], T.ju[:], T.ends[:, r:r + 1], T.dlt[:, r:r + 1],
                        A.is_ge, A.mult).then_inc(sem.f4, 1)
        t.wait_ge(sem.f4, r + 1)
        mm = t.matmul(T.b3[:, 0:128], T.eye[:], T.term[:, 128 * r:128 * r + 128], False, r == 7)
    mm.then_inc(sem.pf, 1)
    v.wait_ge(sem.pf, 1)
    v.tensor_scalar(T.fin[:], T.b3[:, 0:128], float(ZC), None, A.min).then_inc(sem.f9, 1)

    for q in (v, s):
        q.wait_ge(sem.f9, 1)
        q.wait_ge(sem.pk, 2)
        q.wait_ge(sem.pk2, 2)
        q.wait_ge(sem.dpeer, 3 * ne)
        q.wait_ge(sem.down2, nx)
        q.wait_ge(sem.drel, 3 * ne + 3 * n_off + n_on)
    win = T.land[:]
    stores = []
    lo = 0
    for n, w in enumerate(PIECES):
        for q, base in ((v, 0), (s, TX // 2)):
            a, b = base + lo, base + lo + w
            src = win.indirect(T.fin[:, a // 16:b // 16])
            done = sem["y%s%d" % ("v" if q is v else "s", n)]
            if q is v:
                v.tensor_copy(T.yb[:, a:b], src).then_inc(done, 1)
            else:
                s.activation(T.yb[:, a:b], src, COPY).then_inc(done, 1)
            stores.append((a, b, done))
        lo += w
    for k, (a, b, done) in enumerate(stores):
        q = s if k == len(stores) - 1 else g.sync
        q.wait_ge(done, 1)
        q.dma_start(T.y[:, a:b], T.yb[:, a:b]).then_inc(sem.st, 16)
    g.sync.wait_ge(sem.st, 16 * len(stores))
